import numpy as np
import ml_dtypes


def mxq(x, axis, fmt="e4m3"):
    dtype, down = {"e4m3": (ml_dtypes.float8_e4m3fn, 7), "e5m2": (ml_dtypes.float8_e5m2, 14)}[fmt]
    v = np.moveaxis(np.asarray(x, np.float32).astype(ml_dtypes.bfloat16).astype(np.float64), axis, -1)
    blocks = v.reshape(v.shape[:-1] + (-1, 32))
    amax = np.abs(blocks).max(-1, keepdims=True)
    byte = np.maximum(np.where(amax > 0, np.frexp(amax)[1] - 1 + 127, 0) - down, 1)
    scale = np.exp2(byte - 127.0)
    codes = (blocks / scale).astype(np.float32).astype(dtype).astype(np.float64)
    return np.moveaxis((codes * scale).reshape(v.shape), -1, axis)


WIDE = False


def mx_kscale(k):
    if not WIDE:
        return np.ones(k)
    levels = np.array([10, -10, 5, -5, 0])
    if k % 512:
        return np.exp2(np.random.permutation(np.resize(levels, k // 32))).repeat(32)
    a = np.empty((k // 512, 16))
    for p in range(k // 512):
        a[p, :8] = np.random.permutation(np.resize(levels, 8))
        for g in range(8):
            far = levels[np.abs(levels - a[p, g]) >= 10]
            a[p, g + 8] = far[np.random.randint(len(far))]
    return np.exp2(a.ravel()).repeat(32)


def f64(x):
    return np.asarray(x).astype(np.float64)


def striped(idx):
    return np.tile(np.asarray(idx).reshape(-1, 16).T, (8, 1)).astype(np.uint16)


def unstriped(offs):
    return offs[:16].T.reshape(-1).astype(np.int64)


E2M1 = np.array([0.0, 0.5, 1.0, 1.5, 2.0, 3.0, 4.0, 6.0, -0.0, -0.5, -1.0, -1.5, -2.0, -3.0, -4.0, -6.0])


def pack_weight(w, fmt):
    k, n = w.shape
    w = f64(np.asarray(w, np.float32).astype(ml_dtypes.bfloat16)).reshape(k // 32, 32, n)
    amax = np.abs(w).max(1)
    if fmt == "e4m3":
        byte = np.frexp(amax)[1] - 1 + 127 - 7
    else:
        mant, ex = np.frexp(amax / 6.0)
        byte = np.where(mant > 0.5, ex, ex - 1) + 127
    byte = np.clip(np.where(amax > 0, byte, 1), 1, 254)
    scaled = (w * np.exp2(127.0 - byte)[:, None, :]).reshape(k, n).astype(np.float32)
    by_word = np.ascontiguousarray(scaled.reshape(k // 512, 128, 4, n).transpose(0, 1, 3, 2))
    if fmt == "e4m3":
        words = by_word.astype(ml_dtypes.float8_e4m3fn).view(np.uint8)
    else:
        c = by_word.astype(ml_dtypes.float4_e2m1fn).view(np.uint8) & 0xF
        words = (c[..., 0::2] | (c[..., 1::2] << 4)).reshape(k // 512, 128, 2 * n)
    return np.ascontiguousarray(words), np.ascontiguousarray(byte.astype(np.uint8).reshape(k // 512, 16, n))


def unpack_weight(words, scales, fmt):
    g, _, n = scales.shape
    words = np.ascontiguousarray(words).reshape(g, 128, n, -1)
    if fmt == "e4m3":
        vals = words.view(ml_dtypes.float8_e4m3fn).astype(np.float64)
    else:
        nib = np.empty((g, 128, n, 4), np.uint8)
        nib[..., 0::2] = words & 0xF
        nib[..., 1::2] = words >> 4
        vals = E2M1[nib]
    vals = vals * np.repeat(np.exp2(scales.astype(np.float64) - 127.0), 8, axis=1)[..., None]
    return vals.transpose(0, 1, 3, 2).reshape(g * 512, n)


def bf(x):
    return np.asarray(x, np.float32).astype(ml_dtypes.bfloat16)


def planes(Y):
    r, m = Y.shape
    b = f64(bf(Y)).reshape(r // 32, 32, m)
    amax = np.abs(b).max(1)
    byte = np.clip(np.where(amax > 0, np.frexp(amax)[1] - 1 + 127 - 7, 1), 1, 254)
    codes = (b * np.exp2(127.0 - byte)[:, None, :]).reshape(r, m).astype(np.float32).astype(ml_dtypes.float8_e4m3fn).view(np.uint8)
    words = codes.reshape(r // 512, 128, 4, m).transpose(0, 1, 3, 2)
    return np.ascontiguousarray(words), np.ascontiguousarray(byte.astype(np.uint8).reshape(r // 512, 16, m))


K, T, J, N = 1024, 1024, 512, 512


def setup_inputs():
    n = np.random.standard_normal
    idx = np.random.permutation(T)[:J]
    idx2 = np.random.permutation(T)[:J]
    fk = mx_kscale(K)
    wap = pack_weight(n((K, N)) * 1 / np.sqrt(K) * fk[:, None], "e2m1")
    wbp = pack_weight(n((K, N)) * 1 / np.sqrt(K) * fk[:, None], "e4m3")
    return {
        "xt": (n((K, T)) / fk[:, None]).astype(np.float32),
        "wa_words": wap[0],
        "wa_scales": wap[1],
        "wb_words": wbp[0],
        "wb_scales": wbp[1],
        "ga": (np.random.uniform(0.4, 1.2, (1, J))).astype(np.float32),
        "offs": striped(idx),
        "offs2": striped(idx2),
    }


def reference(xt, wa_words, wa_scales, wb_words, wb_scales, ga, offs, offs2):
    idx = unstriped(offs)
    idx2 = unstriped(offs2)
    wau = unpack_weight(wa_words, wa_scales, "e2m1")
    wbu = unpack_weight(wb_words, wb_scales, "e4m3")
    xtidxq = mxq(f64(xt)[:, idx], 0, "e4m3")
    a = wau.T @ xtidxq
    xtidx2q = mxq(f64(xt)[:, idx2], 0, "e4m3")
    b = wbu.T @ xtidx2q
    y = f64(ga) * a * b / (np.abs(a) + np.abs(b) + 0.2)
    words, scales = planes(y)
    return y, words, scales

@@ -1,0 +1,213 @@
+from contextlib import ExitStack
+
+import concourse.mybir as mybir
+from concourse.masks import make_identity
+
+K, T, J, N = 1024, 1024, 512, 512
+FLOPS = 2 * 2 * K * J * N
+
+F32 = mybir.dt.float32
+BF16 = mybir.dt.bfloat16
+I32 = mybir.dt.int32
+U32 = mybir.dt.uint32
+U16 = mybir.dt.uint16
+U8 = mybir.dt.uint8
+FP8X4 = mybir.dt.float8_e4m3fn_x4
+FP4X4 = mybir.dt.float4_e2m1fn_x4
+ACT = mybir.ActivationFunctionType
+MULT = mybir.AluOpType.mult
+ADD = mybir.AluOpType.add
+
+P = 128
+PASSES = 2
+CHUNK = 512
+TILES = J // P
+COPY_ON_VECTOR = (2, 3)
+
+
+def tile_moe_experts_product_over_sizes_pl_kernel(
+    tc, xt, wa_words, wa_scales, wb_words, wb_scales, ga, offs, offs2, out_0, out_1, out_2
+):
+    nc = tc.nc
+    with ExitStack() as ctx:
+        keep = ctx.enter_context(tc.tile_pool(name="keep", bufs=1))
+        work = ctx.enter_context(tc.tile_pool(name="work", bufs=4))
+        psum = ctx.enter_context(tc.psum_pool(name="psum", bufs=1))
+
+        one = keep.tile([P, 1], F32)
+        warm = keep.tile([P, 1], F32)
+        nc.vector.memset(one[:], 1.0)
+        nc.scalar.activation(warm[:], one[:], ACT.Abs_reciprocal_sqrt)
+        lists = [keep.tile([P, J // 16], U16, name=f"list{l}") for l in range(2)]
+        x_rows = xt.rearrange("(g p u e) t -> g u p e t", g=PASSES, u=2, e=2)
+        wa = keep.tile([P, PASSES, 2 * N], U8, align_bytes=64)
+        wb = keep.tile([P, PASSES, 4 * N], U8, align_bytes=64)
+        w_scales = [keep.tile([P, PASSES, N], U8, align_bytes=64, name=f"w_scale{l}") for l in range(2)]
+        gate = keep.tile([P, TILES], F32)
+        for l in range(2):
+            nc.gpsimd.memset(w_scales[l][:].bitcast(I32), 0)
+        raw = {}
+
+        def load_plane(plane):
+            for c in range(T // CHUNK):
+                raw[plane, c] = keep.tile([P, 2, CHUNK], F32, align_bytes=64, tag=f"raw{plane}_{c}", name=f"raw{plane}_{c}")
+                nc.sync.dma_start(raw[plane, c][:], x_rows[plane // 2, plane % 2, :, :, c * CHUNK : (c + 1) * CHUNK])
+
+        def load_scales(tile, source):
+            for q in range(4):
+                nc.sync.dma_start(
+                    tile[32 * q : 32 * q + 4, :, :].bitcast(I32),
+                    source[:, 4 * q : 4 * q + 4, :].rearrange("z r c -> r z c").bitcast(I32),
+                )
+
+        load_plane(0)
+        nc.sync.dma_start(lists[0][:], offs)
+        nc.sync.dma_start(lists[1][:], offs2)
+        load_plane(1)
+        load_plane(2)
+        load_scales(w_scales[0], wa_scales)
+        load_plane(3)
+        load_scales(w_scales[1], wb_scales)
+        nc.sync.dma_start(wa[:].bitcast(I32), wa_words.rearrange("z p c -> p z c").bitcast(I32))
+        nc.sync.dma_start(wb[:].bitcast(I32), wb_words.rearrange("z p c r -> p z (c r)").bitcast(I32))
+        with nc.allow_non_contiguous_dma(reason="one gate value a partition and slot tile"):
+            nc.sync.dma_start(gate[:], ga.rearrange("o (i p) -> p (o i)", p=P))
+
+        ident = keep.tile([P, P], F32)
+        make_identity(nc, ident[:])
+
+        pairs = [keep.tile([P, T], F32, name=f"pairs{plane}") for plane in range(4)]
+        picked0 = keep.tile([P, 4, J], F32)
+        picked1 = keep.tile([P, 2, J + P], F32)
+        codes = [keep.tile([P, PASSES, 2 * P], U32, align_bytes=64, name=f"codes{i}") for i in range(TILES)]
+        scales = [keep.tile([P, PASSES, 2 * P], U8, align_bytes=64, name=f"scales{i}") for i in range(TILES)]
+        y_codes = keep.tile([P, J], U32, align_bytes=64)
+        y_scales = keep.tile([P, J], U8, align_bytes=64)
+        banks = {(l, i): psum.tile([P, N], F32, tag=f"bank{l}_{i}", name=f"sum{l}_{i}") for l in range(2) for i in range(TILES)}
+
+        def cast(plane, c, start, stop, on_vector):
+            dst = pairs[plane][:, c * CHUNK + start : c * CHUNK + stop].bitcast(BF16).rearrange("p (t e) -> p t e", e=2)
+            src = raw[plane, c][:, :, start:stop].rearrange("p e t -> p t e")
+            if on_vector:
+                nc.vector.tensor_copy(dst, src)
+            else:
+                nc.scalar.activation(dst, src, ACT.Copy)
+
+        def gather(plane, start, stop, tile, row, column):
+            for l in range(2):
+                nc.vector.tensor_copy(
+                    tile[:, row + l, column : column + stop - start],
+                    pairs[plane][:].indirect(lists[l][:, start // 16 : stop // 16]),
+                )
+
+        def woven_part(i, g0, g1):
+            return woven[:, (PASSES * i + g0) * 4 * P : (PASSES * i + g1) * 4 * P]
+
+        def quantize(i, g0, g1):
+            nc.vector.quantize_mx(
+                out=codes[i][:, g0:g1, :].rearrange("p g c -> p (g c)").bitcast(FP8X4),
+                scales=scales[i][:, g0:g1, :].rearrange("p g c -> p (g c)"),
+                in_=woven_part(i, g0, g1).bitcast(BF16),
+            )
+
+        def multiply(i, l, g):
+            w, dtype = ((wa, FP4X4), (wb, FP8X4))[l]
+            nc.tensor.matmul_mx(
+                out=banks[l, i][:],
+                lhsT=codes[i][:, g, l * P : (l + 1) * P].bitcast(FP8X4),
+                lhsT_scale=scales[i][:, g, l * P : (l + 1) * P],
+                rhs=w[:, g, :].bitcast(dtype),
+                rhs_scale=w_scales[l][:, g, :],
+                start=(g == 0),
+                stop=(g == PASSES - 1),
+            )
+
+        def weave_first_pass(i):
+            src = picked0[:, :, i * P : (i + 1) * P].rearrange("p (u l) j -> p l j u", u=2)
+            nc.scalar.copy(woven_part(i, 0, 1).rearrange("p (l j u) -> p l j u", l=2, u=2), src)
+
+        def second_pass(i):
+            gather(3, i * P, (i + 1) * P, picked1, 0, J)
+            src = picked1[:].rearrange("p l (c j) -> p l j c", j=P)[:, :, :, i : TILES + 1 : TILES - i]
+            nc.vector.tensor_copy(woven_part(i, 1, 2).rearrange("p (l j u) -> p l j u", l=2, u=2), src)
+            if i == 0:
+                quantize(i, 1, 2)
+                for l in range(2):
+                    multiply(i, l, 1)
+            else:
+                quantize(i, 0, 2)
+                for l in range(2):
+                    for g in range(PASSES):
+                        multiply(i, l, g)
+
+        def slots_side(i):
+            a, b = (banks[l, i][:].rearrange("j (m t) -> j t m", t=4) for l in range(2))
+            a_tile = work.tile([P, 4, P], F32)
+            a_copy = a_tile[:]
+            a_abs = work.tile([P, 4, P], F32)
+            b_abs = work.tile([P, 4, P], F32)
+            if i == 0:
+                prod = woven_part(TILES - 1, 1, 2).rearrange("p (t m) -> p t m", t=4)
+            else:
+                prod_tile = work.tile([P, 4, P], F32)
+                prod = prod_tile[:]
+            nc.scalar.activation(a_abs[:], a, ACT.Abs)
+            if i in COPY_ON_VECTOR:
+                nc.vector.tensor_copy(a_copy, a)
+            else:
+                nc.scalar.copy(a_copy, a)
+            nc.scalar.activation(b_abs[:], b, ACT.Abs)
+            nc.vector.scalar_tensor_tensor(prod, b, gate[:, i : i + 1], a_copy, MULT, MULT)
+            size = psum.tile([P, 4, P], F32, tag=f"bank0_{i}", name=f"size{i}")
+            prod_t = psum.tile([P, 4, P], F32, tag=f"bank1_{i}", name=f"prod_t{i}")
+            for t in range(4):
+                nc.tensor.matmul(size[:, t, :], a_abs[:, t, :], ident[:], start=True, stop=False, is_transpose=True)
+                nc.tensor.matmul(size[:, t, :], b_abs[:, t, :], ident[:], start=False, stop=True, is_transpose=True)
+            for t in range(4):
+                nc.tensor.transpose(prod_t[:, t, :], prod[:, t, :], ident[:])
+            return size, prod_t
+
+        def features_side(i, size, prod_t):
+            cols = slice(i * P, (i + 1) * P)
+            square = work.tile([P, 4, P], F32)
+            inverse = work.tile([P, 4, P], F32)
+            y = work.tile([P, 4, P], F32)
+            y_bf16 = work.tile([P, P, 4], BF16, align_bytes=64)
+            nc.scalar.activation(square[:], size[:], ACT.Square, bias=0.2)
+            nc.scalar.activation(inverse[:], square[:], ACT.Abs_reciprocal_sqrt)
+            nc.vector.tensor_tensor(y[:], prod_t[:], inverse[:], MULT)
+            nc.sync.dma_start(out_0.rearrange("(p t) j -> p t j", t=4)[:, :, cols], y[:])
+            nc.vector.tensor_copy(y_bf16[:], y[:].rearrange("p t j -> p j t"))
+            nc.vector.quantize_mx(
+                out=y_codes[:, cols].bitcast(FP8X4),
+                scales=y_scales[:, cols],
+                in_=y_bf16[:].rearrange("p j t -> p (j t)"),
+            )
+            nc.sync.dma_start(
+                out_1[0].rearrange("p c r -> p (c r)").bitcast(I32)[:, cols], y_codes[:, cols].bitcast(I32)
+            )
+
+        for plane in range(4):
+            for c in range(T // CHUNK):
+                cast(plane, c, 0, CHUNK, plane == 0)
+            if plane < 2:
+                gather(plane, 0, J, picked0, 2 * plane, 0)
+            if plane == 2:
+                gather(plane, 0, J, picked1, 0, 0)
+        woven = keep.tile([P, TILES * PASSES * 4 * P], F32, align_bytes=64, tag="raw3_1", name="woven")
+        weave_first_pass(0)
+        quantize(0, 0, 1)
+        for l in range(2):
+            multiply(0, l, 0)
+        second_pass(0)
+        for i in range(1, TILES):
+            weave_first_pass(i)
+            second_pass(i)
+        turned = {0: slots_side(0)}
+        for i in range(TILES):
+            if i + 1 < TILES:
+                turned[i + 1] = slots_side(i + 1)
+            features_side(i, *turned[i])
+        for q in range(4):
+            queue = nc.sync if q % 2 == 0 else nc.scalar
+            queue.dma_start(out_2[0, 4 * q : 4 * q + 4, :].bitcast(I32), y_scales[32 * q : 32 * q + 4, :].bitcast(I32))

@@ -54,22 +54,20 @@ def tile_moe_experts_product_over_sizes_pl_kernel(
                 nc.sync.dma_start(raw[plane, c][:], x_rows[plane // 2, plane % 2, :, :, c * CHUNK : (c + 1) * CHUNK])
 
         def load_scales(tile, source):
-            for q in range(4):
-                nc.sync.dma_start(
-                    tile[32 * q : 32 * q + 4, :, :].bitcast(I32),
-                    source[:, 4 * q : 4 * q + 4, :].rearrange("z r c -> r z c").bitcast(I32),
-                )
+            rows = source.rearrange("z (q r) c -> r q z c", r=4)
+            for r in range(4):
+                nc.sync.dma_start(tile[r:P:32, :, :].bitcast(I32), rows[r].bitcast(I32))
 
         load_plane(0)
         nc.sync.dma_start(lists[0][:], offs)
         nc.sync.dma_start(lists[1][:], offs2)
         load_plane(1)
         load_plane(2)
-        load_scales(w_scales[0], wa_scales)
         load_plane(3)
-        load_scales(w_scales[1], wb_scales)
         nc.sync.dma_start(wa[:].bitcast(I32), wa_words.rearrange("z p c -> p z c").bitcast(I32))
+        load_scales(w_scales[0], wa_scales)
         nc.sync.dma_start(wb[:].bitcast(I32), wb_words.rearrange("z p c r -> p z (c r)").bitcast(I32))
+        load_scales(w_scales[1], wb_scales)
         with nc.allow_non_contiguous_dma(reason="one gate value a partition and slot tile"):
             nc.sync.dma_start(gate[:], ga.rearrange("o (i p) -> p (o i)", p=P))
 
@@ -122,23 +120,20 @@ def tile_moe_experts_product_over_sizes_pl_kernel(
                 stop=(g == PASSES - 1),
             )
 
-        def weave_first_pass(i):
+        def first_pass(i):
             src = picked0[:, :, i * P : (i + 1) * P].rearrange("p (u l) j -> p l j u", u=2)
             nc.scalar.copy(woven_part(i, 0, 1).rearrange("p (l j u) -> p l j u", l=2, u=2), src)
+            quantize(i, 0, 1)
+            for l in range(2):
+                multiply(i, l, 0)
 
         def second_pass(i):
             gather(3, i * P, (i + 1) * P, picked1, 0, J)
             src = picked1[:].rearrange("p l (c j) -> p l j c", j=P)[:, :, :, i : TILES + 1 : TILES - i]
             nc.vector.tensor_copy(woven_part(i, 1, 2).rearrange("p (l j u) -> p l j u", l=2, u=2), src)
-            if i == 0:
-                quantize(i, 1, 2)
-                for l in range(2):
-                    multiply(i, l, 1)
-            else:
-                quantize(i, 0, 2)
-                for l in range(2):
-                    for g in range(PASSES):
-                        multiply(i, l, g)
+            quantize(i, 1, 2)
+            for l in range(2):
+                multiply(i, l, 1)
 
         def slots_side(i):
             a, b = (banks[l, i][:].rearrange("j (m t) -> j t m", t=4) for l in range(2))
@@ -147,7 +142,7 @@ def tile_moe_experts_product_over_sizes_pl_kernel(
             a_abs = work.tile([P, 4, P], F32)
             b_abs = work.tile([P, 4, P], F32)
             if i == 0:
-                prod = woven_part(TILES - 1, 1, 2).rearrange("p (t m) -> p t m", t=4)
+                prod = woven_part(1, 1, 2).rearrange("p (t m) -> p t m", t=4)
             else:
                 prod_tile = work.tile([P, 4, P], F32)
                 prod = prod_tile[:]
@@ -195,14 +190,13 @@ def tile_moe_experts_product_over_sizes_pl_kernel(
             if plane == 2:
                 gather(plane, 0, J, picked1, 0, 0)
         woven = keep.tile([P, TILES * PASSES * 4 * P], F32, align_bytes=64, tag="raw3_1", name="woven")
-        weave_first_pass(0)
-        quantize(0, 0, 1)
-        for l in range(2):
-            multiply(0, l, 0)
-        second_pass(0)
-        for i in range(1, TILES):
-            weave_first_pass(i)
+        for i in range(2):
+            first_pass(i)
             second_pass(i)
+        first_pass(2)
+        first_pass(3)
+        second_pass(2)
+        second_pass(3)
         turned = {0: slots_side(0)}
         for i in range(TILES):
             if i + 1 < TILES:
@@ -210,4 +204,4 @@ def tile_moe_experts_product_over_sizes_pl_kernel(
             features_side(i, *turned[i])
         for q in range(4):
             queue = nc.sync if q % 2 == 0 else nc.scalar
-            queue.dma_start(out_2[0, 4 * q : 4 * q + 4, :].bitcast(I32), y_scales[32 * q : 32 * q + 4, :].bitcast(I32))
+            queue.dma_start(out_2[0, q:16:4, :].bitcast(I32), y_scales[q:P:32, :].bitcast(I32))

@@ -22,7 +22,8 @@ P = 128
 PASSES = 2
 CHUNK = 512
 TILES = J // P
-COPY_ON_VECTOR = (2, 3)
+FIRST_SHARE = 352
+COPY_ON_VECTOR = (1, 2)
 
 
 def tile_moe_experts_product_over_sizes_pl_kernel(
@@ -76,7 +77,7 @@ def tile_moe_experts_product_over_sizes_pl_kernel(
 
         pairs = [keep.tile([P, T], F32, name=f"pairs{plane}") for plane in range(4)]
         picked0 = keep.tile([P, 4, J], F32)
-        picked1 = keep.tile([P, 2, J + P], F32)
+        picked1 = keep.tile([P, 2, J + 2 * P], F32)
         codes = [keep.tile([P, PASSES, 2 * P], U32, align_bytes=64, name=f"codes{i}") for i in range(TILES)]
         scales = [keep.tile([P, PASSES, 2 * P], U8, align_bytes=64, name=f"scales{i}") for i in range(TILES)]
         y_codes = keep.tile([P, J], U32, align_bytes=64)
@@ -128,9 +129,13 @@ def tile_moe_experts_product_over_sizes_pl_kernel(
                 multiply(i, l, 0)
 
         def second_pass(i):
-            gather(3, i * P, (i + 1) * P, picked1, 0, J)
-            src = picked1[:].rearrange("p l (c j) -> p l j c", j=P)[:, :, :, i : TILES + 1 : TILES - i]
-            nc.vector.tensor_copy(woven_part(i, 1, 2).rearrange("p (l j u) -> p l j u", l=2, u=2), src)
+            slot = TILES + i % 2
+            gather(3, i * P, (i + 1) * P, picked1, 0, slot * P)
+            src = picked1[:].rearrange("p l (c j) -> p l j c", j=P)[:, :, :, i : slot + 1 : slot - i]
+            if i in (0, 1):
+                nc.scalar.copy(woven_part(i, 1, 2).rearrange("p (l j u) -> p l j u", l=2, u=2), src)
+            else:
+                nc.vector.tensor_copy(woven_part(i, 1, 2).rearrange("p (l j u) -> p l j u", l=2, u=2), src)
             quantize(i, 1, 2)
             for l in range(2):
                 multiply(i, l, 1)
@@ -164,27 +169,50 @@ def tile_moe_experts_product_over_sizes_pl_kernel(
 
         def features_side(i, size, prod_t):
             cols = slice(i * P, (i + 1) * P)
-            square = work.tile([P, 4, P], F32)
-            inverse = work.tile([P, 4, P], F32)
             y = work.tile([P, 4, P], F32)
             y_bf16 = work.tile([P, P, 4], BF16, align_bytes=64)
-            nc.scalar.activation(square[:], size[:], ACT.Square, bias=0.2)
-            nc.scalar.activation(inverse[:], square[:], ACT.Abs_reciprocal_sqrt)
-            nc.vector.tensor_tensor(y[:], prod_t[:], inverse[:], MULT)
+            first = work.tile([P, 4, P], F32)
+            second = work.tile([P, 4, P], F32)
+            width = P // 2 if i in (3,) else P
+            parts = [slice(c, c + width) for c in range(0, P, width)]
+            if i in ():
+                for part in parts:
+                    nc.scalar.activation(first[:, :, part], size[:, :, part], ACT.Abs_reciprocal_sqrt, bias=0.2)
+                for part in parts:
+                    nc.vector.tensor_tensor(second[:, :, part], prod_t[:, :, part], first[:, :, part], MULT)
+                for part in parts:
+                    nc.vector.tensor_tensor(y[:, :, part], second[:, :, part], first[:, :, part], MULT)
+            else:
+                for part in parts:
+                    nc.scalar.activation(first[:, :, part], size[:, :, part], ACT.Square, bias=0.2)
+                for part in parts:
+                    nc.scalar.activation(second[:, :, part], first[:, :, part], ACT.Abs_reciprocal_sqrt)
+                for part in parts:
+                    nc.vector.tensor_tensor(y[:, :, part], prod_t[:, :, part], second[:, :, part], MULT)
             nc.sync.dma_start(out_0.rearrange("(p t) j -> p t j", t=4)[:, :, cols], y[:])
-            nc.vector.tensor_copy(y_bf16[:], y[:].rearrange("p t j -> p j t"))
-            nc.vector.quantize_mx(
-                out=y_codes[:, cols].bitcast(FP8X4),
-                scales=y_scales[:, cols],
-                in_=y_bf16[:].rearrange("p j t -> p (j t)"),
-            )
+            for part in parts:
+                if i in ():
+                    nc.gpsimd.tensor_scalar(y_bf16[:, part, :], y[:, :, part].rearrange("p t j -> p j t"), 1.0, -0.0, MULT, ADD)
+                else:
+                    nc.vector.tensor_copy(y_bf16[:, part, :], y[:, :, part].rearrange("p t j -> p j t"))
+            for part in parts:
+                part_cols = slice(i * P + part.start, i * P + part.stop)
+                nc.vector.quantize_mx(
+                    out=y_codes[:, part_cols].bitcast(FP8X4),
+                    scales=y_scales[:, part_cols],
+                    in_=y_bf16[:, part, :].rearrange("p j t -> p (j t)"),
+                )
             nc.sync.dma_start(
                 out_1[0].rearrange("p c r -> p (c r)").bitcast(I32)[:, cols], y_codes[:, cols].bitcast(I32)
             )
 
         for plane in range(4):
-            for c in range(T // CHUNK):
-                cast(plane, c, 0, CHUNK, plane == 0)
+            cast(plane, 0, 0, CHUNK, plane == 0)
+            if plane == 0:
+                cast(plane, 1, 0, FIRST_SHARE, True)
+                cast(plane, 1, FIRST_SHARE, CHUNK, False)
+            else:
+                cast(plane, 1, 0, CHUNK, False)
             if plane < 2:
                 gather(plane, 0, J, picked0, 2 * plane, 0)
             if plane == 2:
@@ -196,8 +224,8 @@ def tile_moe_experts_product_over_sizes_pl_kernel(
         first_pass(2)
         first_pass(3)
         second_pass(2)
-        second_pass(3)
         turned = {0: slots_side(0)}
+        second_pass(3)
         for i in range(TILES):
             if i + 1 < TILES:
                 turned[i + 1] = slots_side(i + 1)

@@ -159,15 +159,15 @@ def tile_moe_experts_product_over_sizes_pl_kernel(
             nc.scalar.activation(b_abs[:], b, ACT.Abs)
             nc.vector.scalar_tensor_tensor(prod, b, gate[:, i : i + 1], a_copy, MULT, MULT)
             size = psum.tile([P, 4, P], F32, tag=f"bank0_{i}", name=f"size{i}")
-            prod_t = psum.tile([P, 4, P], F32, tag=f"bank1_{i}", name=f"prod_t{i}")
             for t in range(4):
                 nc.tensor.matmul(size[:, t, :], a_abs[:, t, :], ident[:], start=True, stop=False, is_transpose=True)
                 nc.tensor.matmul(size[:, t, :], b_abs[:, t, :], ident[:], start=False, stop=True, is_transpose=True)
+            return size, prod
+
+        def features_side(i, size, prod):
+            prod_t = psum.tile([P, 4, P], F32, tag=f"bank1_{i}", name=f"prod_t{i}")
             for t in range(4):
                 nc.tensor.transpose(prod_t[:, t, :], prod[:, t, :], ident[:])
-            return size, prod_t
-
-        def features_side(i, size, prod_t):
             cols = slice(i * P, (i + 1) * P)
             y = work.tile([P, 4, P], F32)
             y_bf16 = work.tile([P, P, 4], BF16, align_bytes=64)

from contextlib import ExitStack

import concourse.mybir as mybir
from concourse.masks import make_identity

K, T, J, N = 1024, 1024, 512, 512
FLOPS = 2 * 2 * K * J * N

F32 = mybir.dt.float32
BF16 = mybir.dt.bfloat16
I32 = mybir.dt.int32
U32 = mybir.dt.uint32
U16 = mybir.dt.uint16
U8 = mybir.dt.uint8
FP8X4 = mybir.dt.float8_e4m3fn_x4
FP4X4 = mybir.dt.float4_e2m1fn_x4
ACT = mybir.ActivationFunctionType
MULT = mybir.AluOpType.mult
ADD = mybir.AluOpType.add

P = 128
PASSES = 2
CHUNK = 512
TILES = J // P
FIRST_SHARE = 352
COPY_ON_VECTOR = (1, 2)


def tile_moe_experts_product_over_sizes_pl_kernel(
    tc, xt, wa_words, wa_scales, wb_words, wb_scales, ga, offs, offs2, out_0, out_1, out_2
):
    nc = tc.nc
    with ExitStack() as ctx:
        keep = ctx.enter_context(tc.tile_pool(name="keep", bufs=1))
        work = ctx.enter_context(tc.tile_pool(name="work", bufs=4))
        psum = ctx.enter_context(tc.psum_pool(name="psum", bufs=1))

        one = keep.tile([P, 1], F32)
        warm = keep.tile([P, 1], F32)
        nc.vector.memset(one[:], 1.0)
        nc.scalar.activation(warm[:], one[:], ACT.Abs_reciprocal_sqrt)
        lists = [keep.tile([P, J // 16], U16, name=f"list{l}") for l in range(2)]
        x_rows = xt.rearrange("(g p u e) t -> g u p e t", g=PASSES, u=2, e=2)
        wa = keep.tile([P, PASSES, 2 * N], U8, align_bytes=64)
        wb = keep.tile([P, PASSES, 4 * N], U8, align_bytes=64)
        w_scales = [keep.tile([P, PASSES, N], U8, align_bytes=64, name=f"w_scale{l}") for l in range(2)]
        gate = keep.tile([P, TILES], F32)
        for l in range(2):
            nc.gpsimd.memset(w_scales[l][:].bitcast(I32), 0)
        raw = {}

        def load_plane(plane):
            for c in range(T // CHUNK):
                raw[plane, c] = keep.tile([P, 2, CHUNK], F32, align_bytes=64, tag=f"raw{plane}_{c}", name=f"raw{plane}_{c}")
                nc.sync.dma_start(raw[plane, c][:], x_rows[plane // 2, plane % 2, :, :, c * CHUNK : (c + 1) * CHUNK])

        def load_scales(tile, source):
            rows = source.rearrange("z (q r) c -> r q z c", r=4)
            for r in range(4):
                nc.sync.dma_start(tile[r:P:32, :, :].bitcast(I32), rows[r].bitcast(I32))

        load_plane(0)
        nc.sync.dma_start(lists[0][:], offs)
        nc.sync.dma_start(lists[1][:], offs2)
        load_plane(1)
        load_plane(2)
        load_plane(3)
        nc.sync.dma_start(wa[:].bitcast(I32), wa_words.rearrange("z p c -> p z c").bitcast(I32))
        load_scales(w_scales[0], wa_scales)
        nc.sync.dma_start(wb[:].bitcast(I32), wb_words.rearrange("z p c r -> p z (c r)").bitcast(I32))
        load_scales(w_scales[1], wb_scales)
        with nc.allow_non_contiguous_dma(reason="one gate value a partition and slot tile"):
            nc.sync.dma_start(gate[:], ga.rearrange("o (i p) -> p (o i)", p=P))

        ident = keep.tile([P, P], F32)
        make_identity(nc, ident[:])

        pairs = [keep.tile([P, T], F32, name=f"pairs{plane}") for plane in range(4)]
        picked0 = keep.tile([P, 4, J], F32)
        picked1 = keep.tile([P, 2, J + 2 * P], F32)
        codes = [keep.tile([P, PASSES, 2 * P], U32, align_bytes=64, name=f"codes{i}") for i in range(TILES)]
        scales = [keep.tile([P, PASSES, 2 * P], U8, align_bytes=64, name=f"scales{i}") for i in range(TILES)]
        y_codes = keep.tile([P, J], U32, align_bytes=64)
        y_scales = keep.tile([P, J], U8, align_bytes=64)
        banks = {(l, i): psum.tile([P, N], F32, tag=f"bank{l}_{i}", name=f"sum{l}_{i}") for l in range(2) for i in range(TILES)}

        def cast(plane, c, start, stop, on_vector):
            dst = pairs[plane][:, c * CHUNK + start : c * CHUNK + stop].bitcast(BF16).rearrange("p (t e) -> p t e", e=2)
            src = raw[plane, c][:, :, start:stop].rearrange("p e t -> p t e")
            if on_vector:
                nc.vector.tensor_copy(dst, src)
            else:
                nc.scalar.activation(dst, src, ACT.Copy)

        def gather(plane, start, stop, tile, row, column):
            for l in range(2):
                nc.vector.tensor_copy(
                    tile[:, row + l, column : column + stop - start],
                    pairs[plane][:].indirect(lists[l][:, start // 16 : stop // 16]),
                )

        def woven_part(i, g0, g1):
            return woven[:, (PASSES * i + g0) * 4 * P : (PASSES * i + g1) * 4 * P]

        def quantize(i, g0, g1):
            nc.vector.quantize_mx(
                out=codes[i][:, g0:g1, :].rearrange("p g c -> p (g c)").bitcast(FP8X4),
                scales=scales[i][:, g0:g1, :].rearrange("p g c -> p (g c)"),
                in_=woven_part(i, g0, g1).bitcast(BF16),
            )

        def multiply(i, l, g):
            w, dtype = ((wa, FP4X4), (wb, FP8X4))[l]
            nc.tensor.matmul_mx(
                out=banks[l, i][:],
                lhsT=codes[i][:, g, l * P : (l + 1) * P].bitcast(FP8X4),
                lhsT_scale=scales[i][:, g, l * P : (l + 1) * P],
                rhs=w[:, g, :].bitcast(dtype),
                rhs_scale=w_scales[l][:, g, :],
                start=(g == 0),
                stop=(g == PASSES - 1),
            )

        def first_pass(i):
            src = picked0[:, :, i * P : (i + 1) * P].rearrange("p (u l) j -> p l j u", u=2)
            nc.scalar.copy(woven_part(i, 0, 1).rearrange("p (l j u) -> p l j u", l=2, u=2), src)
            quantize(i, 0, 1)
            for l in range(2):
                multiply(i, l, 0)

        def second_pass(i):
            slot = TILES + i % 2
            gather(3, i * P, (i + 1) * P, picked1, 0, slot * P)
            src = picked1[:].rearrange("p l (c j) -> p l j c", j=P)[:, :, :, i : slot + 1 : slot - i]
            if i in (0, 1):
                nc.scalar.copy(woven_part(i, 1, 2).rearrange("p (l j u) -> p l j u", l=2, u=2), src)
            else:
                nc.vector.tensor_copy(woven_part(i, 1, 2).rearrange("p (l j u) -> p l j u", l=2, u=2), src)
            quantize(i, 1, 2)
            for l in range(2):
                multiply(i, l, 1)

        def slots_side(i):
            a, b = (banks[l, i][:].rearrange("j (m t) -> j t m", t=4) for l in range(2))
            a_tile = work.tile([P, 4, P], F32)
            a_copy = a_tile[:]
            a_abs = work.tile([P, 4, P], F32)
            b_abs = work.tile([P, 4, P], F32)
            if i == 0:
                prod = woven_part(1, 1, 2).rearrange("p (t m) -> p t m", t=4)
            else:
                prod_tile = work.tile([P, 4, P], F32)
                prod = prod_tile[:]
            nc.scalar.activation(a_abs[:], a, ACT.Abs)
            if i in COPY_ON_VECTOR:
                nc.vector.tensor_copy(a_copy, a)
            else:
                nc.scalar.copy(a_copy, a)
            nc.scalar.activation(b_abs[:], b, ACT.Abs)
            nc.vector.scalar_tensor_tensor(prod, b, gate[:, i : i + 1], a_copy, MULT, MULT)
            size = psum.tile([P, 4, P], F32, tag=f"bank0_{i}", name=f"size{i}")
            for t in range(4):
                nc.tensor.matmul(size[:, t, :], a_abs[:, t, :], ident[:], start=True, stop=False, is_transpose=True)
                nc.tensor.matmul(size[:, t, :], b_abs[:, t, :], ident[:], start=False, stop=True, is_transpose=True)
            return size, prod

        def features_side(i, size, prod):
            prod_t = psum.tile([P, 4, P], F32, tag=f"bank1_{i}", name=f"prod_t{i}")
            for t in range(4):
                nc.tensor.transpose(prod_t[:, t, :], prod[:, t, :], ident[:])
            cols = slice(i * P, (i + 1) * P)
            y = work.tile([P, 4, P], F32)
            y_bf16 = work.tile([P, P, 4], BF16, align_bytes=64)
            first = work.tile([P, 4, P], F32)
            second = work.tile([P, 4, P], F32)
            width = P // 2 if i in (3,) else P
            parts = [slice(c, c + width) for c in range(0, P, width)]
            if i in ():
                for part in parts:
                    nc.scalar.activation(first[:, :, part], size[:, :, part], ACT.Abs_reciprocal_sqrt, bias=0.2)
                for part in parts:
                    nc.vector.tensor_tensor(second[:, :, part], prod_t[:, :, part], first[:, :, part], MULT)
                for part in parts:
                    nc.vector.tensor_tensor(y[:, :, part], second[:, :, part], first[:, :, part], MULT)
            else:
                for part in parts:
                    nc.scalar.activation(first[:, :, part], size[:, :, part], ACT.Square, bias=0.2)
                for part in parts:
                    nc.scalar.activation(second[:, :, part], first[:, :, part], ACT.Abs_reciprocal_sqrt)
                for part in parts:
                    nc.vector.tensor_tensor(y[:, :, part], prod_t[:, :, part], second[:, :, part], MULT)
            nc.sync.dma_start(out_0.rearrange("(p t) j -> p t j", t=4)[:, :, cols], y[:])
            for part in parts:
                if i in ():
                    nc.gpsimd.tensor_scalar(y_bf16[:, part, :], y[:, :, part].rearrange("p t j -> p j t"), 1.0, -0.0, MULT, ADD)
                else:
                    nc.vector.tensor_copy(y_bf16[:, part, :], y[:, :, part].rearrange("p t j -> p j t"))
            for part in parts:
                part_cols = slice(i * P + part.start, i * P + part.stop)
                nc.vector.quantize_mx(
                    out=y_codes[:, part_cols].bitcast(FP8X4),
                    scales=y_scales[:, part_cols],
                    in_=y_bf16[:, part, :].rearrange("p j t -> p (j t)"),
                )
            nc.sync.dma_start(
                out_1[0].rearrange("p c r -> p (c r)").bitcast(I32)[:, cols], y_codes[:, cols].bitcast(I32)
            )

        for plane in range(4):
            cast(plane, 0, 0, CHUNK, plane == 0)
            if plane == 0:
                cast(plane, 1, 0, FIRST_SHARE, True)
                cast(plane, 1, FIRST_SHARE, CHUNK, False)
            else:
                cast(plane, 1, 0, CHUNK, False)
            if plane < 2:
                gather(plane, 0, J, picked0, 2 * plane, 0)
            if plane == 2:
                gather(plane, 0, J, picked1, 0, 0)
        woven = keep.tile([P, TILES * PASSES * 4 * P], F32, align_bytes=64, tag="raw3_1", name="woven")
        for i in range(2):
            first_pass(i)
            second_pass(i)
        first_pass(2)
        first_pass(3)
        second_pass(2)
        turned = {0: slots_side(0)}
        second_pass(3)
        for i in range(TILES):
            if i + 1 < TILES:
                turned[i + 1] = slots_side(i + 1)
            features_side(i, *turned[i])
        for q in range(4):
            queue = nc.sync if q % 2 == 0 else nc.scalar
            queue.dma_start(out_2[0, q:16:4, :].bitcast(I32), y_scales[q:P:32, :].bitcast(I32))
